import numpy as np
import ml_dtypes


def mxq(x, axis, fmt="e4m3"):
    dtype, down = {"e4m3": (ml_dtypes.float8_e4m3fn, 7), "e5m2": (ml_dtypes.float8_e5m2, 14)}[fmt]
    v = np.moveaxis(np.asarray(x, np.float32).astype(ml_dtypes.bfloat16).astype(np.float64), axis, -1)
    blocks = v.reshape(v.shape[:-1] + (-1, 32))
    amax = np.abs(blocks).max(-1, keepdims=True)
    byte = np.maximum(np.where(amax > 0, np.frexp(amax)[1] - 1 + 127, 0) - down, 1)
    scale = np.exp2(byte - 127.0)
    codes = (blocks / scale).astype(np.float32).astype(dtype).astype(np.float64)
    return np.moveaxis((codes * scale).reshape(v.shape), -1, axis)


WIDE = False


def mx_kscale(k):
    if not WIDE:
        return np.ones(k)
    levels = np.array([10, -10, 5, -5, 0])
    if k % 512:
        return np.exp2(np.random.permutation(np.resize(levels, k // 32))).repeat(32)
    a = np.empty((k // 512, 16))
    for p in range(k // 512):
        a[p, :8] = np.random.permutation(np.resize(levels, 8))
        for g in range(8):
            far = levels[np.abs(levels - a[p, g]) >= 10]
            a[p, g + 8] = far[np.random.randint(len(far))]
    return np.exp2(a.ravel()).repeat(32)


BF16 = ml_dtypes.bfloat16


def bf(x):
    return np.asarray(x, np.float32).astype(BF16)


def f64(x):
    return np.asarray(x).astype(np.float64)


E2M1 = np.array([0.0, 0.5, 1.0, 1.5, 2.0, 3.0, 4.0, 6.0, -0.0, -0.5, -1.0, -1.5, -2.0, -3.0, -4.0, -6.0])


def pack_weight(w, fmt):
    k, n = w.shape
    w = f64(bf(w)).reshape(k // 32, 32, n)
    amax = np.abs(w).max(1)
    if fmt == "e4m3":
        byte = np.frexp(amax)[1] - 1 + 127 - 7
    else:
        mant, ex = np.frexp(amax / 6.0)
        byte = np.where(mant > 0.5, ex, ex - 1) + 127
    byte = np.clip(np.where(amax > 0, byte, 1), 1, 254)
    scaled = (w * np.exp2(127.0 - byte)[:, None, :]).reshape(k, n).astype(np.float32)
    by_word = np.ascontiguousarray(scaled.reshape(k // 512, 128, 4, n).transpose(0, 1, 3, 2))
    if fmt == "e4m3":
        words = by_word.astype(ml_dtypes.float8_e4m3fn).view(np.uint8)
    else:
        c = by_word.astype(ml_dtypes.float4_e2m1fn).view(np.uint8) & 0xF
        words = c[..., 0::2] | (c[..., 1::2] << 4)
    return np.ascontiguousarray(words), np.ascontiguousarray(byte.astype(np.uint8).reshape(k // 512, 16, n))


def unpack_weight(words, scales, fmt):
    g, p, n, _ = words.shape
    if fmt == "e4m3":
        vals = np.ascontiguousarray(words).view(ml_dtypes.float8_e4m3fn).astype(np.float64)
    else:
        nib = np.empty((g, p, n, 4), np.uint8)
        nib[..., 0::2] = words & 0xF
        nib[..., 1::2] = words >> 4
        vals = E2M1[nib]
    vals = vals * np.repeat(np.exp2(scales.astype(np.float64) - 127.0), 8, axis=1)[..., None]
    return vals.transpose(0, 1, 3, 2).reshape(g * 512, n)
def pack4(w):
    words, scales = pack_weight(w, "e2m1")
    return words.reshape(words.shape[0], 128, -1), scales


def unpack4(words, scales):
    return unpack_weight(words.reshape(words.shape[0], 128, -1, 2), scales, "e2m1")


def planes(Y):
    n, m = Y.shape
    b = f64(bf(Y)).reshape(n // 32, 32, m)
    amax = np.abs(b).max(1)
    byte = np.clip(np.where(amax > 0, np.frexp(amax)[1] - 1 + 127 - 7, 1), 1, 254)
    codes = (b * np.exp2(127.0 - byte)[:, None, :]).reshape(n, m).astype(np.float32).astype(ml_dtypes.float8_e4m3fn).view(np.uint8)
    words = codes.reshape(n // 512, 128, 4, m).transpose(0, 1, 3, 2)
    return np.ascontiguousarray(words), np.ascontiguousarray(byte.astype(np.uint8).reshape(n // 512, 16, m))


B, T, L, F, Q = 4, 512, 1024, 512, 2


def setup_inputs():
    s, t = mx_kscale(L), mx_kscale(T)
    x = bf(np.random.standard_normal((B, T, L)) * s)
    bank = bf(np.random.standard_normal((Q, L, F)) * 0.4 / np.sqrt(L) / s[None, :, None])
    smoother = np.random.standard_normal((T, T)) * 0.45 / np.sqrt(T) / t[None, :]
    words, scales = pack4(smoother.T)
    return {
        "x": x,
        "bank": bank,
        "smoother_words": words,
        "smoother_scales": scales,
        "tgain": bf((1.0 + 0.3 * np.random.standard_normal(T)) * t),
        "alpha": bf(np.random.uniform(0.6, 1.0, F)),
        "delta": bf(np.random.uniform(1.0, 3.0, F)),
        "root": bf(np.random.uniform(0.3, 0.7, F)),
    }


def quadrature_energy(x, bank):
    xq = mxq(x, 2, "e4m3")
    zr = xq @ mxq(bank[0], 0, "e4m3")
    zi = xq @ mxq(bank[1], 0, "e4m3")
    return zr * zr + zi * zi


def smoothed_level(en, smoother, tgain):
    mb = np.mean(en, axis=1, keepdims=True)
    c = (en - mb) * tgain[None, :, None]
    sm = smoother @ mxq(c, 1, "e4m3")
    return np.maximum(mb + sm, 0.1)


def core(x, bank, smoother_words, smoother_scales, tgain, alpha, delta, root):
    x, bank, tgain = f64(x), f64(bank), f64(tgain)
    smoother = unpack4(smoother_words, smoother_scales).T
    alpha, delta, root = f64(alpha), f64(delta), f64(root)
    en = quadrature_energy(x, bank)
    m = smoothed_level(en, smoother, tgain)
    p = en / np.power(0.01 + m, alpha)
    o = np.power(p + delta, root) - np.power(delta, root)
    return o


def reference(x, bank, smoother_words, smoother_scales, tgain, alpha, delta, root):
    R_out = core(x, bank, smoother_words, smoother_scales, tgain, alpha, delta, root)
    words, scales = planes(np.moveaxis(R_out, 1, 0).reshape(512, -1))
    return R_out, words, scales

@@ -1,0 +1,467 @@
+from contextlib import ExitStack
+
+import concourse.mybir as mybir
+from concourse.masks import make_identity
+
+B, T, L, F = 4, 512, 1024, 512
+FLOPS = 2 * B * T * L * F * 2 + 2 * B * T * T * F
+
+F32 = mybir.dt.float32
+BF16 = mybir.dt.bfloat16
+I32 = mybir.dt.int32
+U32 = mybir.dt.uint32
+U8 = mybir.dt.uint8
+FP8X4 = mybir.dt.float8_e4m3fn_x4
+FP4X4 = mybir.dt.float4_e2m1fn_x4
+ACT = mybir.ActivationFunctionType
+ALU = mybir.AluOpType
+
+P = 128
+PACK = 4
+PASSES = L // (P * PACK)
+FT = F // P
+UNITS = B * FT
+GROUP_ENDS = (8, 16)
+SCALAR_RATE = 1
+VECTOR_RATE = 2
+SCALAR_X_COPIES = 11
+SCALAR_INTERLEAVES = 0
+TAIL_ENGINE = (0, 0, 0, 0, 0, 0, 1, 0)
+DRAIN_RATE = 2
+HEAD_SCALAR = 1
+HALF = F // 2
+
+
+def tile_learnedquadraturebankpcensmoother_x2_kernel(
+    tc, x, bank, smoother_words, smoother_scales, tgain, alpha, delta, root, out_0, out_1, out_2
+):
+    nc = tc.nc
+    with ExitStack() as ctx:
+        keep = ctx.enter_context(tc.tile_pool(name="keep", bufs=1))
+        work = ctx.enter_context(tc.tile_pool(name="work", bufs=3))
+        psum = ctx.enter_context(tc.psum_pool(name="psum", bufs=8))
+        ctx.enter_context(tc.manual_schedule())
+
+        def kept(name, shape, dtype):
+            return keep.tile(shape, dtype, name=name, tag=name, align_bytes=64)
+
+        def passing(name, shape, dtype, bufs):
+            return work.tile(shape, dtype, name=name, tag=name, bufs=bufs, align_bytes=64)
+
+        def psum_bank():
+            return psum.tile([P, T], F32, name="psum_bank", tag="psum_bank")
+
+        x_raw = {}
+        bank_raw = {}
+
+        def load_x(b, pairs):
+            rows = x[b].rearrange("(p j) l -> p j l", j=PACK)
+            tile = kept("x_raw_%d_%d" % (b, pairs[0]), [P, 2 * len(pairs), L], BF16)
+            nc.sync.dma_start(out=tile[:], in_=rows[:, 2 * pairs[0] : 2 * pairs[-1] + 2, :])
+            for n, pair in enumerate(pairs):
+                x_raw[b, pair] = tile[:, 2 * n : 2 * n + 2, :]
+
+        def load_bank(q, g, h):
+            tile = kept("bank_raw_%d_%d_%d" % (q, g, h), [P, PACK, HALF], BF16)
+            rows = bank[q, g * P * PACK : (g + 1) * P * PACK, h * HALF : (h + 1) * HALF]
+            nc.sync.dma_start(out=tile[:], in_=rows.rearrange("(p j) f -> p j f", j=PACK))
+            bank_raw[q, g, h] = tile
+
+        ident = kept("ident", [P, P], F32)
+        make_identity(nc, ident[:])
+        w_scales = kept("w_scales", [P, T], U8)
+        nc.gpsimd.memset(w_scales[:].bitcast(I32), 0)
+        band_rows = kept("band_rows", [P, P], F32)
+        nc.gpsimd.memset(band_rows[:], 0.0)
+        warm = kept("warm", [P, 1], F32)
+        nc.scalar.activation(out=warm[:], in_=ident[:, 0:1], func=ACT.Ln, bias=1.0)
+
+        load_x(0, [0])
+        load_x(0, [1])
+        for h in range(2):
+            for q in range(2):
+                for g in range(PASSES):
+                    load_bank(q, g, h)
+        gain_raw = kept("gain_raw", [P, PACK], BF16)
+        nc.sync.dma_start(out=gain_raw[:], in_=tgain.rearrange("(p j) -> p j", j=PACK))
+        w_words = kept("w_words", [P, 2 * T], U8)
+        nc.sync.dma_start(out=w_words[:].bitcast(I32), in_=smoother_words[0].bitcast(I32))
+        load_x(1, [0, 1])
+        for quad in range(4):
+            nc.sync.dma_start(
+                out=w_scales[32 * quad : 32 * quad + 4, :].bitcast(I32),
+                in_=smoother_scales[0, 4 * quad : 4 * quad + 4, :].bitcast(I32),
+            )
+        band_raw = kept("band_raw", [3 * FT, P], BF16)
+        for n, vec in enumerate((alpha, delta, root)):
+            nc.sync.dma_start(out=band_raw[FT * n : FT * (n + 1), :], in_=vec.rearrange("(c m) -> c m", m=P))
+        load_x(2, [0, 1])
+        load_x(3, [0, 1])
+
+        bank_codes, bank_scales, bank_grouped = {}, {}, {}
+
+        def interleave(grouped, src, on_scalar):
+            dst = grouped[:].rearrange("p (c i) j -> p c j i", i=4)
+            src = src[:].rearrange("p j (c i) -> p c j i", i=4)
+            if on_scalar == 2:
+                nc.gpsimd.tensor_scalar(out=dst, in0=src, scalar1=1.0, scalar2=0.0, op0=ALU.mult, op1=ALU.add)
+            elif on_scalar:
+                nc.scalar.copy(out=dst, in_=src)
+            else:
+                nc.vector.tensor_copy(out=dst, in_=src)
+
+        def bank_interleave(q, g, h, on_scalar):
+            grouped = passing("bank_grouped", [P, HALF, PACK], BF16, 4)
+            interleave(grouped, bank_raw[q, g, h], on_scalar)
+            bank_grouped[q, g, h] = grouped
+
+        def bank_quantize(q, g, h):
+            codes = kept("bank_codes_%d_%d_%d" % (q, g, h), [P, HALF], U32)
+            scales = kept("bank_scales_%d_%d_%d" % (q, g, h), [P, HALF], U8)
+            nc.vector.quantize_mx(
+                out=codes[:].bitcast(FP8X4),
+                scales=scales[:],
+                in_=bank_grouped[q, g, h][:].rearrange("p c j -> p (c j)"),
+            )
+            bank_codes[q, g, h], bank_scales[q, g, h] = codes, scales
+
+        x_turned, x_grouped, x_codes, x_scales = {}, {}, {}, {}
+
+        def x_transpose(b, g, pair):
+            turned = psum_bank()
+            for jj in range(2):
+                words = x_raw[b, pair][:, jj, :].bitcast(F32)
+                for u in range(2):
+                    slot = 2 * jj + u
+                    nc.tensor.transpose(
+                        turned[:, slot * P : (slot + 1) * P],
+                        words[:, 2 * P * g + u : 2 * P * (g + 1) : 2],
+                        ident[:],
+                    )
+            x_turned[b, g, pair] = turned
+
+        def x_copy(b, g, pair, on_scalar):
+            if pair == 0:
+                x_grouped[b, g] = passing("x_grouped", [P, T * PACK], BF16, 3)
+            words = x_grouped[b, g][:].bitcast(F32)
+            dst = words[:, pair * T : (pair + 1) * T].rearrange("p (j r u) -> p j r u", j=2, u=2)
+            src = x_turned[b, g, pair][:].rearrange("p (j u r) -> p j r u", j=2, u=2)
+            if on_scalar:
+                nc.scalar.copy(out=dst, in_=src)
+            else:
+                nc.vector.tensor_copy(out=dst, in_=src)
+
+        def x_quantize(b, g):
+            codes = kept("x_codes_%d_%d" % (b, g), [P, T], U32)
+            scales = kept("x_scales_%d_%d" % (b, g), [P, T], U8)
+            nc.vector.quantize_mx(out=codes[:].bitcast(FP8X4), scales=scales[:], in_=x_grouped[b, g][:])
+            x_codes[b, g], x_scales[b, g] = codes, scales
+
+        sums = kept("sums", [P, UNITS, 2], F32)
+        mean = kept("mean", [P, UNITS], F32)
+        squares = {}
+
+        def project_and_square(u, q):
+            b, ft = divmod(u, FT)
+            h, cols = ft // 2, slice((ft % 2) * P, (ft % 2 + 1) * P)
+            z = psum_bank()
+            for g in range(PASSES):
+                nc.tensor.matmul_mx(
+                    out=z[:],
+                    lhsT=bank_codes[q, g, h][:, cols].bitcast(FP8X4),
+                    lhsT_scale=bank_scales[q, g, h][:, cols],
+                    rhs=x_codes[b, g][:].bitcast(FP8X4),
+                    rhs_scale=x_scales[b, g][:],
+                    start=(g == 0),
+                    stop=(g == PASSES - 1),
+                )
+            square = passing("square_%d" % q, [P, T], F32, 5)
+            nc.scalar.activation(out=square[:], in_=z[:], func=ACT.Square, accum_out=sums[:, u, q : q + 1])
+            squares[u, q] = square
+
+        def time_mean(u):
+            nc.vector.tensor_scalar(
+                out=mean[:, u : u + 1], in0=sums[:, u, 0:1], scalar1=sums[:, u, 1:2], scalar2=1.0 / T,
+                op0=ALU.add, op1=ALU.mult,
+            )
+
+        dev = [kept("dev_%d" % ft, [P, B, T], F32) for ft in range(FT)]
+        chain = [kept("chain_%d" % ft, [P, B, T], F32) for ft in range(FT)]
+
+        def of_unit(tiles, u):
+            b, ft = divmod(u, FT)
+            return tiles[ft][:, b, :]
+
+        def deviation(u):
+            nc.vector.scalar_tensor_tensor(
+                out=of_unit(dev, u), in0=squares[u, 0][:], scalar=mean[:, u : u + 1], in1=squares[u, 1][:],
+                op0=ALU.subtract, op1=ALU.add,
+            )
+
+        dev_turned, c_grouped, c_codes, c_scales, smooth = {}, {}, {}, {}, {}
+
+        def turn(src):
+            turned = psum_bank()
+            for j in range(PACK):
+                nc.tensor.transpose(turned[:, j * P : (j + 1) * P], src[:, j * P : (j + 1) * P], ident[:])
+            return turned
+
+        def dev_transpose(u):
+            dev_turned[u] = turn(of_unit(dev, u))
+
+        gain = kept("gain", [P, P, PACK], F32)
+
+        def gain_setup():
+            nc.vector.tensor_copy(out=gain[:], in_=gain_raw[:].unsqueeze(1).to_broadcast([P, P, PACK]))
+
+        def c_round(u):
+            grouped = passing("c_grouped", [P, P, PACK], BF16, 3)
+            nc.vector.tensor_tensor(
+                out=grouped[:], in0=dev_turned[u][:].rearrange("p (j f) -> p f j", j=PACK), in1=gain[:], op=ALU.mult
+            )
+            c_grouped[u] = grouped
+
+        def c_quantize(u):
+            codes = passing("c_codes", [P, P], U32, 3)
+            scales = passing("c_scales", [P, P], U8, 3)
+            nc.vector.quantize_mx(
+                out=codes[:].bitcast(FP8X4), scales=scales[:], in_=c_grouped[u][:].rearrange("p f j -> p (f j)")
+            )
+            c_codes[u], c_scales[u] = codes, scales
+
+        def smooth_matmul(u):
+            sm = psum_bank()
+            nc.tensor.matmul_mx(
+                out=sm[:], lhsT=c_codes[u][:].bitcast(FP8X4), lhsT_scale=c_scales[u][:],
+                rhs=w_words[:].bitcast(FP4X4), rhs_scale=w_scales[:], start=True, stop=True,
+            )
+            smooth[u] = sm
+
+        def level(u):
+            nc.vector.tensor_scalar(
+                out=of_unit(chain, u).rearrange("f (j p) -> f j p", j=PACK),
+                in0=smooth[u][:].rearrange("f (p j) -> f j p", j=PACK),
+                scalar1=mean[:, u : u + 1], scalar2=0.1, op0=ALU.add, op1=ALU.max,
+            )
+
+        def log_level(u):
+            nc.scalar.activation(out=of_unit(chain, u), in_=of_unit(chain, u), func=ACT.Ln, bias=0.01)
+
+        band = kept("band", [P, 3 * FT], F32)
+        neg_alpha = kept("neg_alpha", [P, FT], F32)
+        log_delta = kept("log_delta", [P, FT], F32)
+        root_log_delta = kept("root_log_delta", [P, FT], F32)
+        offset_col = kept("offset_col", [P, FT], F32)
+        offset_row = kept("offset_row", [P, F], F32)
+
+        def band_setup():
+            nc.vector.tensor_copy(out=band_rows[0 : 3 * FT, :], in_=band_raw[:])
+            turned = psum_bank()
+            nc.tensor.transpose(turned[:, 0:P], band_rows[:], ident[:])
+            nc.vector.tensor_copy(out=band[:], in_=turned[:, 0 : 3 * FT])
+            nc.scalar.activation(out=log_delta[:], in_=band[:, FT : 2 * FT], func=ACT.Ln)
+            nc.vector.tensor_scalar(out=neg_alpha[:], in0=band[:, 0:FT], scalar1=-1.0, scalar2=None, op0=ALU.mult)
+            nc.vector.tensor_tensor(out=root_log_delta[:], in0=log_delta[:], in1=band[:, 2 * FT : 3 * FT], op=ALU.mult)
+
+        def offset_setup():
+            turned = psum_bank()
+            for ft in range(FT):
+                nc.tensor.transpose(
+                    turned[:, ft * P : (ft + 1) * P], offset_col[:, ft : ft + 1].to_broadcast([P, P]), ident[:]
+                )
+            nc.vector.tensor_copy(out=offset_row[:], in_=turned[:])
+
+        def chain_of(units):
+            return chain[units[0] % FT][:, units[0] // FT : units[-1] // FT + 1, :]
+
+        def inverse_power(units):
+            ft = units[0] % FT
+            nc.scalar.activation(out=chain_of(units), in_=chain_of(units), func=ACT.Exp, scale=neg_alpha[:, ft : ft + 1])
+
+        def normalise(u):
+            nc.vector.scalar_tensor_tensor(
+                out=of_unit(chain, u), in0=of_unit(dev, u), scalar=mean[:, u : u + 1], in1=of_unit(chain, u),
+                op0=ALU.add, op1=ALU.mult,
+            )
+
+        def log_shifted(units):
+            col = FT + units[0] % FT
+            nc.scalar.activation(out=chain_of(units), in_=chain_of(units), func=ACT.Ln, bias=band[:, col : col + 1])
+
+        def root_power(units):
+            col = 2 * FT + units[0] % FT
+            nc.scalar.activation(out=chain_of(units), in_=chain_of(units), func=ACT.Exp, scale=band[:, col : col + 1])
+
+        result, result_turned, result_grouped = {}, {}, {}
+        out_scales = kept("out_scales", [P, B * F], U8)
+        out_words = out_1[0].rearrange("p m t -> p (m t)").bitcast(I32)
+
+        def result_transpose(u):
+            result_turned[u] = turn(of_unit(chain, u))
+
+        def result_subtract(u):
+            b, ft = divmod(u, FT)
+            if (b, ft // 2) not in result:
+                result[b, ft // 2] = passing("result", [P, PACK, HALF], F32, 4)
+            nc.vector.tensor_tensor(
+                out=result[b, ft // 2][:, :, (ft % 2) * P : (ft % 2 + 1) * P],
+                in0=result_turned[u][:].rearrange("p (j f) -> p j f", j=PACK),
+                in1=offset_row[:, ft * P : (ft + 1) * P].unsqueeze(1).to_broadcast([P, PACK, P]),
+                op=ALU.subtract,
+            )
+
+        def result_store(b, h):
+            rows = out_0[b].rearrange("(p j) f -> p j f", j=PACK)
+            nc.sync.dma_start(out=rows[:, :, h * HALF : (h + 1) * HALF], in_=result[b, h][:])
+
+        def result_interleave(b, h, on_scalar):
+            grouped = passing("result_grouped", [P, HALF, PACK], BF16, 3)
+            interleave(grouped, result[b, h], on_scalar)
+            result_grouped[b, h] = grouped
+
+        def result_quantize(b, h):
+            cols = slice(b * F + h * HALF, b * F + (h + 1) * HALF)
+            codes = passing("result_codes", [P, HALF], U32, 4)
+            nc.vector.quantize_mx(
+                out=codes[:].bitcast(FP8X4), scales=out_scales[:, cols],
+                in_=result_grouped[b, h][:].rearrange("p c j -> p (c j)"),
+            )
+            nc.sync.dma_start(out=out_words[:, cols], in_=codes[:].bitcast(I32))
+
+        for pair in range(2):
+            for g in range(PASSES):
+                x_transpose(0, g, pair)
+                x_copy(0, g, pair, True)
+        bank_interleave(0, 0, 0, False)
+        x_quantize(0, 0)
+        bank_interleave(0, 1, 0, False)
+        bank_quantize(0, 0, 0)
+        x_quantize(0, 1)
+        bank_quantize(0, 1, 0)
+        bank_interleave(1, 0, 0, HEAD_SCALAR >= 1)
+        bank_interleave(1, 1, 0, False)
+        bank_quantize(1, 0, 0)
+        bank_quantize(1, 1, 0)
+        late_bank = [(q, g) for q in range(2) for g in range(PASSES)]
+        x_pieces = [(b, g, pair) for b in range(1, B) for g in range(PASSES) for pair in range(2)]
+
+        def x_pieces_of(step):
+            return [piece for n, piece in enumerate(x_pieces) if (1 + n // 2 if n < 4 else n - 1) == step]
+
+        groups = [list(range(lo, hi)) for lo, hi in zip((0,) + GROUP_ENDS[:-1], GROUP_ENDS)]
+
+        def runs(units, width):
+            found = []
+            for first in range(0, B, width):
+                for ft in range(FT):
+                    run = [u for u in units if u % FT == ft and first <= u // FT < first + width]
+                    if run:
+                        found.append(run)
+            return found
+
+        scalar_list = []
+        for n in range(len(groups) + 1):
+            if n < len(groups):
+                scalar_list.extend(("log_level", [u]) for u in groups[n])
+            if n >= 1:
+                scalar_list.extend(("log_shifted", run) for run in runs(groups[n - 1], 2))
+            if n < len(groups):
+                scalar_list.extend(("inverse_power", run) for run in runs(groups[n], 2))
+            if n >= 1:
+                scalar_list.extend(("root_power", run) for run in runs(groups[n - 1], 1 if n == len(groups) else 2))
+
+        levelled, normalised = set(), set()
+        to_normalise, to_turn, to_group, to_quantize = [], [], [], []
+        subtracted = set()
+        step = 0
+        offset_made = []
+        while step < UNITS + 4 or scalar_list or to_normalise or to_turn or to_group or to_quantize:
+            turning = to_turn[:VECTOR_RATE]
+            to_turn = to_turn[VECTOR_RATE:]
+            if 0 <= step - 3 < UNITS:
+                smooth_matmul(step - 3)
+            if step < UNITS:
+                project_and_square(step, 0)
+                project_and_square(step, 1)
+            for u in turning:
+                result_transpose(u)
+            if step < 2:
+                for n in range(2 * step, 2 * step + 2):
+                    bank_interleave(late_bank[n][0], late_bank[n][1], 1, n < SCALAR_INTERLEAVES)
+            if step == 1:
+                gain_setup()
+            if 0 <= step - 1 < UNITS:
+                time_mean(step - 1)
+            if 0 <= step - 2 < UNITS:
+                c_round(step - 2)
+            if 0 <= step - 1 < UNITS:
+                deviation(step - 1)
+            if step < 2:
+                for n in range(2 * step, 2 * step + 2):
+                    bank_quantize(late_bank[n][0], late_bank[n][1], 1)
+            if 0 <= step - 3 < UNITS:
+                level(step - 3)
+                levelled.add(step - 3)
+            for b, g, pair in x_pieces_of(step):
+                x_transpose(b, g, pair)
+            if 0 <= step - 1 < UNITS:
+                dev_transpose(step - 1)
+            if 0 <= step - 2 < UNITS:
+                c_quantize(step - 2)
+            for b, g, pair in x_pieces_of(step - 1):
+                if pair == 1:
+                    x_quantize(b, g)
+            for b, h in to_quantize:
+                result_quantize(b, h)
+            to_quantize = []
+            for u in to_normalise:
+                normalise(u)
+                normalised.add(u)
+            to_normalise = []
+            for b, h in to_group:
+                result_interleave(b, h, TAIL_ENGINE[2 * b + h])
+                to_quantize.append((b, h))
+            to_group = []
+            for u in turning:
+                result_subtract(u)
+                subtracted.add(u)
+                if u ^ 1 in subtracted:
+                    result_store(u // FT, (u % FT) // 2)
+                    to_group.append((u // FT, (u % FT) // 2))
+            if step == 3:
+                band_setup()
+            if offset_made and step == offset_made[0] + 2:
+                offset_setup()
+            budget = SCALAR_RATE if step < UNITS else DRAIN_RATE
+            while scalar_list and budget > 0:
+                at = 0
+                while scalar_list[at][0] == "log_level" and scalar_list[at][1][0] not in levelled:
+                    at = at + 1
+                kind, run = scalar_list[at]
+                if at > 0 and kind != "log_shifted":
+                    break
+                if kind == "log_level":
+                    log_level(run[0])
+                elif kind == "inverse_power":
+                    if not offset_made:
+                        nc.scalar.activation(out=offset_col[:], in_=root_log_delta[:], func=ACT.Exp)
+                        offset_made.append(step)
+                    inverse_power(run)
+                    to_normalise.extend(run)
+                elif kind == "log_shifted":
+                    if not all(u in normalised for u in run):
+                        break
+                    log_shifted(run)
+                else:
+                    root_power(run)
+                    to_turn.extend(run)
+                budget = budget - len(run)
+                scalar_list = scalar_list[:at] + scalar_list[at + 1 :]
+            for b, g, pair in x_pieces_of(step):
+                x_copy(b, g, pair, step < SCALAR_X_COPIES)
+            step = step + 1
+        for quad in range(4):
+            nc.scalar.dma_start(
+                out=out_2[0, 4 * quad : 4 * quad + 4, :].bitcast(I32),
+                in_=out_scales[32 * quad : 32 * quad + 4, :].bitcast(I32),
+            )

@@ -21,14 +21,14 @@ PACK = 4
 PASSES = L // (P * PACK)
 FT = F // P
 UNITS = B * FT
-GROUP_ENDS = (8, 16)
-SCALAR_RATE = 1
+GROUP_ENDS = (5, 12, 16)
+SCALAR_RATE = 3
 VECTOR_RATE = 2
-SCALAR_X_COPIES = 11
+SCALAR_X_COPIES = 7
 SCALAR_INTERLEAVES = 0
 TAIL_ENGINE = (0, 0, 0, 0, 0, 0, 1, 0)
 DRAIN_RATE = 2
-HEAD_SCALAR = 1
+HS = (1, 0, 0, 0)
 HALF = F // 2
 
 
@@ -40,7 +40,7 @@ def tile_learnedquadraturebankpcensmoother_x2_kernel(
         keep = ctx.enter_context(tc.tile_pool(name="keep", bufs=1))
         work = ctx.enter_context(tc.tile_pool(name="work", bufs=3))
         psum = ctx.enter_context(tc.psum_pool(name="psum", bufs=8))
-        ctx.enter_context(tc.manual_schedule())
+        ctx.enter_context(tc.manual_schedule(engines={mybir.EngineType.Activation, mybir.EngineType.SP, mybir.EngineType.Pool}))
 
         def kept(name, shape, dtype):
             return keep.tile(shape, dtype, name=name, tag=name, align_bytes=64)
@@ -61,11 +61,11 @@ def tile_learnedquadraturebankpcensmoother_x2_kernel(
             for n, pair in enumerate(pairs):
                 x_raw[b, pair] = tile[:, 2 * n : 2 * n + 2, :]
 
-        def load_bank(q, g, h):
-            tile = kept("bank_raw_%d_%d_%d" % (q, g, h), [P, PACK, HALF], BF16)
-            rows = bank[q, g * P * PACK : (g + 1) * P * PACK, h * HALF : (h + 1) * HALF]
+        def load_bank(q, g):
+            tile = kept("bank_raw_%d_%d" % (q, g), [P, PACK, F], BF16)
+            rows = bank[q, g * P * PACK : (g + 1) * P * PACK, :]
             nc.sync.dma_start(out=tile[:], in_=rows.rearrange("(p j) f -> p j f", j=PACK))
-            bank_raw[q, g, h] = tile
+            bank_raw[q, g] = tile
 
         ident = kept("ident", [P, P], F32)
         make_identity(nc, ident[:])
@@ -78,10 +78,9 @@ def tile_learnedquadraturebankpcensmoother_x2_kernel(
 
         load_x(0, [0])
         load_x(0, [1])
-        for h in range(2):
-            for q in range(2):
-                for g in range(PASSES):
-                    load_bank(q, g, h)
+        for q in range(2):
+            for g in range(PASSES):
+                load_bank(q, g)
         gain_raw = kept("gain_raw", [P, PACK], BF16)
         nc.sync.dma_start(out=gain_raw[:], in_=tgain.rearrange("(p j) -> p j", j=PACK))
         w_words = kept("w_words", [P, 2 * T], U8)
@@ -102,7 +101,7 @@ def tile_learnedquadraturebankpcensmoother_x2_kernel(
 
         def interleave(grouped, src, on_scalar):
             dst = grouped[:].rearrange("p (c i) j -> p c j i", i=4)
-            src = src[:].rearrange("p j (c i) -> p c j i", i=4)
+            src = src.rearrange("p j (c i) -> p c j i", i=4)
             if on_scalar == 2:
                 nc.gpsimd.tensor_scalar(out=dst, in0=src, scalar1=1.0, scalar2=0.0, op0=ALU.mult, op1=ALU.add)
             elif on_scalar:
@@ -112,7 +111,7 @@ def tile_learnedquadraturebankpcensmoother_x2_kernel(
 
         def bank_interleave(q, g, h, on_scalar):
             grouped = passing("bank_grouped", [P, HALF, PACK], BF16, 4)
-            interleave(grouped, bank_raw[q, g, h], on_scalar)
+            interleave(grouped, bank_raw[q, g][:, :, h * HALF : (h + 1) * HALF], on_scalar)
             bank_grouped[q, g, h] = grouped
 
         def bank_quantize(q, g, h):
@@ -209,15 +208,12 @@ def tile_learnedquadraturebankpcensmoother_x2_kernel(
         def dev_transpose(u):
             dev_turned[u] = turn(of_unit(dev, u))
 
-        gain = kept("gain", [P, P, PACK], F32)
-
-        def gain_setup():
-            nc.vector.tensor_copy(out=gain[:], in_=gain_raw[:].unsqueeze(1).to_broadcast([P, P, PACK]))
+        gain = gain_raw[:].unsqueeze(1).to_broadcast([P, P, PACK])
 
         def c_round(u):
             grouped = passing("c_grouped", [P, P, PACK], BF16, 3)
             nc.vector.tensor_tensor(
-                out=grouped[:], in0=dev_turned[u][:].rearrange("p (j f) -> p f j", j=PACK), in1=gain[:], op=ALU.mult
+                out=grouped[:], in0=dev_turned[u][:].rearrange("p (j f) -> p f j", j=PACK), in1=gain, op=ALU.mult
             )
             c_grouped[u] = grouped
 
@@ -254,14 +250,23 @@ def tile_learnedquadraturebankpcensmoother_x2_kernel(
         offset_col = kept("offset_col", [P, FT], F32)
         offset_row = kept("offset_row", [P, F], F32)
 
-        def band_setup():
-            nc.vector.tensor_copy(out=band_rows[0 : 3 * FT, :], in_=band_raw[:])
-            turned = psum_bank()
-            nc.tensor.transpose(turned[:, 0:P], band_rows[:], ident[:])
-            nc.vector.tensor_copy(out=band[:], in_=turned[:, 0 : 3 * FT])
-            nc.scalar.activation(out=log_delta[:], in_=band[:, FT : 2 * FT], func=ACT.Ln)
-            nc.vector.tensor_scalar(out=neg_alpha[:], in0=band[:, 0:FT], scalar1=-1.0, scalar2=None, op0=ALU.mult)
-            nc.vector.tensor_tensor(out=root_log_delta[:], in0=log_delta[:], in1=band[:, 2 * FT : 3 * FT], op=ALU.mult)
+        band_turned = []
+
+        def band_setup(stage):
+            if stage == 0:
+                nc.vector.tensor_copy(out=band_rows[0 : 3 * FT, :], in_=band_raw[:])
+            if stage == 1:
+                band_turned.append(psum_bank())
+                nc.tensor.transpose(band_turned[0][:, 0:P], band_rows[:], ident[:])
+            if stage == 2:
+                nc.vector.tensor_copy(out=band[:], in_=band_turned[0][:, 0 : 3 * FT])
+            if stage == 3:
+                nc.scalar.activation(out=log_delta[:], in_=band[:, FT : 2 * FT], func=ACT.Ln)
+                nc.vector.tensor_scalar(out=neg_alpha[:], in0=band[:, 0:FT], scalar1=-1.0, scalar2=None, op0=ALU.mult)
+            if stage == 4:
+                nc.vector.tensor_tensor(
+                    out=root_log_delta[:], in0=log_delta[:], in1=band[:, 2 * FT : 3 * FT], op=ALU.mult
+                )
 
         def offset_setup():
             turned = psum_bank()
@@ -316,7 +321,7 @@ def tile_learnedquadraturebankpcensmoother_x2_kernel(
 
         def result_interleave(b, h, on_scalar):
             grouped = passing("result_grouped", [P, HALF, PACK], BF16, 3)
-            interleave(grouped, result[b, h], on_scalar)
+            interleave(grouped, result[b, h][:], on_scalar)
             result_grouped[b, h] = grouped
 
         def result_quantize(b, h):
@@ -334,15 +339,20 @@ def tile_learnedquadraturebankpcensmoother_x2_kernel(
                 x_copy(0, g, pair, True)
         bank_interleave(0, 0, 0, False)
         x_quantize(0, 0)
-        bank_interleave(0, 1, 0, False)
         bank_quantize(0, 0, 0)
         x_quantize(0, 1)
+        bank_interleave(0, 0, 1, HS[0])
+        bank_interleave(0, 1, 0, False)
         bank_quantize(0, 1, 0)
-        bank_interleave(1, 0, 0, HEAD_SCALAR >= 1)
-        bank_interleave(1, 1, 0, False)
+        project_and_square(0, 0)
+        project_and_square(1, 0)
+        bank_interleave(1, 0, 0, False)
+        bank_quantize(0, 0, 1)
+        bank_interleave(0, 1, 1, HS[1])
         bank_quantize(1, 0, 0)
+        bank_interleave(1, 1, 0, False)
         bank_quantize(1, 1, 0)
-        late_bank = [(q, g) for q in range(2) for g in range(PASSES)]
+        bank_quantize(0, 1, 1)
         x_pieces = [(b, g, pair) for b in range(1, B) for g in range(PASSES) for pair in range(2)]
 
         def x_pieces_of(step):
@@ -352,7 +362,7 @@ def tile_learnedquadraturebankpcensmoother_x2_kernel(
 
         def runs(units, width):
             found = []
-            for first in range(0, B, width):
+            for first in range(units[0] // FT, B, width):
                 for ft in range(FT):
                     run = [u for u in units if u % FT == ft and first <= u // FT < first + width]
                     if run:
@@ -378,18 +388,16 @@ def tile_learnedquadraturebankpcensmoother_x2_kernel(
         while step < UNITS + 4 or scalar_list or to_normalise or to_turn or to_group or to_quantize:
             turning = to_turn[:VECTOR_RATE]
             to_turn = to_turn[VECTOR_RATE:]
+            if step < UNITS:
+                if step >= 2:
+                    project_and_square(step, 0)
+                project_and_square(step, 1)
             if 0 <= step - 3 < UNITS:
                 smooth_matmul(step - 3)
-            if step < UNITS:
-                project_and_square(step, 0)
-                project_and_square(step, 1)
             for u in turning:
                 result_transpose(u)
             if step < 2:
-                for n in range(2 * step, 2 * step + 2):
-                    bank_interleave(late_bank[n][0], late_bank[n][1], 1, n < SCALAR_INTERLEAVES)
-            if step == 1:
-                gain_setup()
+                bank_interleave(1, step, 1, HS[2 + step])
             if 0 <= step - 1 < UNITS:
                 time_mean(step - 1)
             if 0 <= step - 2 < UNITS:
@@ -397,8 +405,7 @@ def tile_learnedquadraturebankpcensmoother_x2_kernel(
             if 0 <= step - 1 < UNITS:
                 deviation(step - 1)
             if step < 2:
-                for n in range(2 * step, 2 * step + 2):
-                    bank_quantize(late_bank[n][0], late_bank[n][1], 1)
+                bank_quantize(1, step, 1)
             if 0 <= step - 3 < UNITS:
                 level(step - 3)
                 levelled.add(step - 3)
@@ -428,8 +435,7 @@ def tile_learnedquadraturebankpcensmoother_x2_kernel(
                 if u ^ 1 in subtracted:
                     result_store(u // FT, (u % FT) // 2)
                     to_group.append((u // FT, (u % FT) // 2))
-            if step == 3:
-                band_setup()
+            band_setup(step - 1)
             if offset_made and step == offset_made[0] + 2:
                 offset_setup()
             budget = SCALAR_RATE if step < UNITS else DRAIN_RATE

@@ -28,7 +28,7 @@ SCALAR_X_COPIES = 7
 SCALAR_INTERLEAVES = 0
 TAIL_ENGINE = (0, 0, 0, 0, 0, 0, 1, 0)
 DRAIN_RATE = 2
-HS = (1, 0, 0, 0)
+WARM = (4, 6)
 HALF = F // 2
 
 
@@ -40,7 +40,7 @@ def tile_learnedquadraturebankpcensmoother_x2_kernel(
         keep = ctx.enter_context(tc.tile_pool(name="keep", bufs=1))
         work = ctx.enter_context(tc.tile_pool(name="work", bufs=3))
         psum = ctx.enter_context(tc.psum_pool(name="psum", bufs=8))
-        ctx.enter_context(tc.manual_schedule(engines={mybir.EngineType.Activation, mybir.EngineType.SP, mybir.EngineType.Pool}))
+        ctx.enter_context(tc.manual_schedule())
 
         def kept(name, shape, dtype):
             return keep.tile(shape, dtype, name=name, tag=name, align_bytes=64)
@@ -76,16 +76,25 @@ def tile_learnedquadraturebankpcensmoother_x2_kernel(
         warm = kept("warm", [P, 1], F32)
         nc.scalar.activation(out=warm[:], in_=ident[:, 0:1], func=ACT.Ln, bias=1.0)
 
+        warm_tile = kept("warm_tile", [P, T], BF16)
+        nc.vector.memset(warm_tile[:], 0.0)
+
+        def warm_tensor(count):
+            scratch = psum_bank()
+            for n in range(count):
+                nc.tensor.matmul(scratch[:], lhsT=warm_tile[:, 0:P], rhs=warm_tile[:], start=True, stop=True)
+
+        warm_tensor(WARM[0])
         load_x(0, [0])
         load_x(0, [1])
         for q in range(2):
             for g in range(PASSES):
                 load_bank(q, g)
+        load_x(1, [0, 1])
         gain_raw = kept("gain_raw", [P, PACK], BF16)
         nc.sync.dma_start(out=gain_raw[:], in_=tgain.rearrange("(p j) -> p j", j=PACK))
         w_words = kept("w_words", [P, 2 * T], U8)
         nc.sync.dma_start(out=w_words[:].bitcast(I32), in_=smoother_words[0].bitcast(I32))
-        load_x(1, [0, 1])
         for quad in range(4):
             nc.sync.dma_start(
                 out=w_scales[32 * quad : 32 * quad + 4, :].bitcast(I32),
@@ -110,7 +119,7 @@ def tile_learnedquadraturebankpcensmoother_x2_kernel(
                 nc.vector.tensor_copy(out=dst, in_=src)
 
         def bank_interleave(q, g, h, on_scalar):
-            grouped = passing("bank_grouped", [P, HALF, PACK], BF16, 4)
+            grouped = passing("bank_grouped", [P, HALF, PACK], BF16, 5)
             interleave(grouped, bank_raw[q, g][:, :, h * HALF : (h + 1) * HALF], on_scalar)
             bank_grouped[q, g, h] = grouped
 
@@ -337,22 +346,27 @@ def tile_learnedquadraturebankpcensmoother_x2_kernel(
             for g in range(PASSES):
                 x_transpose(0, g, pair)
                 x_copy(0, g, pair, True)
+        warm_tensor(WARM[1])
         bank_interleave(0, 0, 0, False)
+        bank_interleave(0, 0, 1, True)
         x_quantize(0, 0)
+        bank_interleave(0, 1, 0, False)
+        bank_interleave(0, 1, 1, True)
         bank_quantize(0, 0, 0)
         x_quantize(0, 1)
-        bank_interleave(0, 0, 1, HS[0])
-        bank_interleave(0, 1, 0, False)
         bank_quantize(0, 1, 0)
         project_and_square(0, 0)
         project_and_square(1, 0)
         bank_interleave(1, 0, 0, False)
         bank_quantize(0, 0, 1)
-        bank_interleave(0, 1, 1, HS[1])
-        bank_quantize(1, 0, 0)
         bank_interleave(1, 1, 0, False)
-        bank_quantize(1, 1, 0)
+        bank_quantize(1, 0, 0)
         bank_quantize(0, 1, 1)
+        bank_interleave(1, 0, 1, True)
+        bank_quantize(1, 1, 0)
+        bank_interleave(1, 1, 1, False)
+        bank_quantize(1, 0, 1)
+        bank_quantize(1, 1, 1)
         x_pieces = [(b, g, pair) for b in range(1, B) for g in range(PASSES) for pair in range(2)]
 
         def x_pieces_of(step):
@@ -396,16 +410,12 @@ def tile_learnedquadraturebankpcensmoother_x2_kernel(
                 smooth_matmul(step - 3)
             for u in turning:
                 result_transpose(u)
-            if step < 2:
-                bank_interleave(1, step, 1, HS[2 + step])
             if 0 <= step - 1 < UNITS:
                 time_mean(step - 1)
             if 0 <= step - 2 < UNITS:
                 c_round(step - 2)
             if 0 <= step - 1 < UNITS:
                 deviation(step - 1)
-            if step < 2:
-                bank_quantize(1, step, 1)
             if 0 <= step - 3 < UNITS:
                 level(step - 3)
                 levelled.add(step - 3)

@@ -22,13 +22,18 @@ PASSES = L // (P * PACK)
 FT = F // P
 UNITS = B * FT
 GROUP_ENDS = (5, 12, 16)
-SCALAR_RATE = 3
+SCALAR_RATE = 2
 VECTOR_RATE = 2
 SCALAR_X_COPIES = 7
 SCALAR_INTERLEAVES = 0
 TAIL_ENGINE = (0, 0, 0, 0, 0, 0, 1, 0)
 DRAIN_RATE = 2
-WARM = (4, 6)
+VECTOR_SQUARES_FROM = 12
+POST_FROM = 19
+TENSOR_SUMS_FROM = 8
+ENERGY_STEP = 21
+WARM = (6, 4)
+H2 = True
 HALF = F // 2
 
 
@@ -85,11 +90,12 @@ def tile_learnedquadraturebankpcensmoother_x2_kernel(
                 nc.tensor.matmul(scratch[:], lhsT=warm_tile[:, 0:P], rhs=warm_tile[:], start=True, stop=True)
 
         warm_tensor(WARM[0])
+        load_bank(0, 0)
         load_x(0, [0])
         load_x(0, [1])
-        for q in range(2):
-            for g in range(PASSES):
-                load_bank(q, g)
+        load_bank(0, 1)
+        load_bank(1, 0)
+        load_bank(1, 1)
         load_x(1, [0, 1])
         gain_raw = kept("gain_raw", [P, PACK], BF16)
         nc.sync.dma_start(out=gain_raw[:], in_=tgain.rearrange("(p j) -> p j", j=PACK))
@@ -165,9 +171,17 @@ def tile_learnedquadraturebankpcensmoother_x2_kernel(
             nc.vector.quantize_mx(out=codes[:].bitcast(FP8X4), scales=scales[:], in_=x_grouped[b, g][:])
             x_codes[b, g], x_scales[b, g] = codes, scales
 
+        dev = [kept("dev_%d" % ft, [P, B, T], F32) for ft in range(FT)]
+        chain = [kept("chain_%d" % ft, [P, B, T], F32) for ft in range(FT)]
+
+        def of_unit(tiles, u):
+            b, ft = divmod(u, FT)
+            return tiles[ft][:, b, :]
+
         sums = kept("sums", [P, UNITS, 2], F32)
-        mean = kept("mean", [P, UNITS], F32)
-        squares = {}
+        neg_mean = kept("neg_mean", [P, UNITS], F32)
+        vector_sums = kept("vector_sums", [P, UNITS], F32)
+        squares, projected, plain = {}, {}, {}
 
         def project_and_square(u, q):
             b, ft = divmod(u, FT)
@@ -183,27 +197,38 @@ def tile_learnedquadraturebankpcensmoother_x2_kernel(
                     start=(g == 0),
                     stop=(g == PASSES - 1),
                 )
-            square = passing("square_%d" % q, [P, T], F32, 5)
-            nc.scalar.activation(out=square[:], in_=z[:], func=ACT.Square, accum_out=sums[:, u, q : q + 1])
+            if u < TENSOR_SUMS_FROM:
+                square = passing("square_%d" % q, [P, T], F32, 3)[:]
+            elif q == 0:
+                square = of_unit(dev, u)
+            else:
+                square = kept("late_square_%d" % u, [P, T], F32)[:]
+            if q == 1 and u >= VECTOR_SQUARES_FROM:
+                projected[u] = z
+            else:
+                nc.scalar.activation(out=square, in_=z[:], func=ACT.Square, accum_out=sums[:, u, q : q + 1])
             squares[u, q] = square
+
+        def vector_copy(u):
+            plain[u] = passing("plain", [P, T], F32, 2)
+            nc.vector.tensor_copy(out=plain[u][:], in_=projected[u][:])
+
+        def vector_square(u):
+            nc.vector.scalar_tensor_tensor(
+                out=squares[u, 1], in0=projected[u][:], scalar=1.0, in1=plain[u][:], op0=ALU.mult, op1=ALU.mult,
+                accum_out=vector_sums[:, u : u + 1],
+            )
 
         def time_mean(u):
             nc.vector.tensor_scalar(
-                out=mean[:, u : u + 1], in0=sums[:, u, 0:1], scalar1=sums[:, u, 1:2], scalar2=1.0 / T,
+                out=neg_mean[:, u : u + 1], in0=sums[:, u, 0:1], scalar1=vector_sums[:, u : u + 1] if u >= VECTOR_SQUARES_FROM else sums[:, u, 1:2], scalar2=-1.0 / T,
                 op0=ALU.add, op1=ALU.mult,
             )
 
-        dev = [kept("dev_%d" % ft, [P, B, T], F32) for ft in range(FT)]
-        chain = [kept("chain_%d" % ft, [P, B, T], F32) for ft in range(FT)]
-
-        def of_unit(tiles, u):
-            b, ft = divmod(u, FT)
-            return tiles[ft][:, b, :]
-
         def deviation(u):
             nc.vector.scalar_tensor_tensor(
-                out=of_unit(dev, u), in0=squares[u, 0][:], scalar=mean[:, u : u + 1], in1=squares[u, 1][:],
-                op0=ALU.subtract, op1=ALU.add,
+                out=of_unit(dev, u), in0=squares[u, 0], scalar=neg_mean[:, u : u + 1], in1=squares[u, 1],
+                op0=ALU.add, op1=ALU.add,
             )
 
         dev_turned, c_grouped, c_codes, c_scales, smooth = {}, {}, {}, {}, {}
@@ -215,7 +240,18 @@ def tile_learnedquadraturebankpcensmoother_x2_kernel(
             return turned
 
         def dev_transpose(u):
-            dev_turned[u] = turn(of_unit(dev, u))
+            if u < TENSOR_SUMS_FROM:
+                dev_turned[u] = turn(of_unit(dev, u))
+                return
+            dev_turned[u] = psum_bank()
+            for j in range(PACK):
+                cols = slice(j * P, (j + 1) * P)
+                terms = (squares[u, 0][:, cols], squares[u, 1][:, cols], neg_mean[:, u : u + 1].to_broadcast([P, P]))
+                for n, term in enumerate(terms):
+                    nc.tensor.matmul(
+                        dev_turned[u][:, cols], lhsT=term, rhs=ident[:], is_transpose=True,
+                        start=(n == 0), stop=(n == len(terms) - 1),
+                    )
 
         gain = gain_raw[:].unsqueeze(1).to_broadcast([P, P, PACK])
 
@@ -246,7 +282,7 @@ def tile_learnedquadraturebankpcensmoother_x2_kernel(
             nc.vector.tensor_scalar(
                 out=of_unit(chain, u).rearrange("f (j p) -> f j p", j=PACK),
                 in0=smooth[u][:].rearrange("f (p j) -> f j p", j=PACK),
-                scalar1=mean[:, u : u + 1], scalar2=0.1, op0=ALU.add, op1=ALU.max,
+                scalar1=neg_mean[:, u : u + 1], scalar2=0.1, op0=ALU.subtract, op1=ALU.max,
             )
 
         def log_level(u):
@@ -292,11 +328,17 @@ def tile_learnedquadraturebankpcensmoother_x2_kernel(
             ft = units[0] % FT
             nc.scalar.activation(out=chain_of(units), in_=chain_of(units), func=ACT.Exp, scale=neg_alpha[:, ft : ft + 1])
 
+        def energy(u):
+            nc.vector.tensor_tensor(out=of_unit(dev, u), in0=of_unit(dev, u), in1=squares[u, 1], op=ALU.add)
+
         def normalise(u):
-            nc.vector.scalar_tensor_tensor(
-                out=of_unit(chain, u), in0=of_unit(dev, u), scalar=mean[:, u : u + 1], in1=of_unit(chain, u),
-                op0=ALU.add, op1=ALU.mult,
-            )
+            if u >= TENSOR_SUMS_FROM:
+                nc.vector.tensor_tensor(out=of_unit(chain, u), in0=of_unit(dev, u), in1=of_unit(chain, u), op=ALU.mult)
+            else:
+                nc.vector.scalar_tensor_tensor(
+                    out=of_unit(chain, u), in0=of_unit(dev, u), scalar=neg_mean[:, u : u + 1], in1=of_unit(chain, u),
+                    op0=ALU.subtract, op1=ALU.mult,
+                )
 
         def log_shifted(units):
             col = FT + units[0] % FT
@@ -342,28 +384,35 @@ def tile_learnedquadraturebankpcensmoother_x2_kernel(
             )
             nc.sync.dma_start(out=out_words[:, cols], in_=codes[:].bitcast(I32))
 
+        def store_scales(queue, cols):
+            for quad in range(4):
+                queue.dma_start(
+                    out=out_2[0, 4 * quad : 4 * quad + 4, cols].bitcast(I32),
+                    in_=out_scales[32 * quad : 32 * quad + 4, cols].bitcast(I32),
+                )
+
+        for h in range(2):
+            bank_interleave(0, 0, h, False)
+        for h in range(2):
+            bank_quantize(0, 0, h)
         for pair in range(2):
             for g in range(PASSES):
                 x_transpose(0, g, pair)
                 x_copy(0, g, pair, True)
         warm_tensor(WARM[1])
-        bank_interleave(0, 0, 0, False)
-        bank_interleave(0, 0, 1, True)
-        x_quantize(0, 0)
         bank_interleave(0, 1, 0, False)
         bank_interleave(0, 1, 1, True)
-        bank_quantize(0, 0, 0)
-        x_quantize(0, 1)
+        x_quantize(0, 0)
         bank_quantize(0, 1, 0)
+        x_quantize(0, 1)
         project_and_square(0, 0)
         project_and_square(1, 0)
         bank_interleave(1, 0, 0, False)
-        bank_quantize(0, 0, 1)
         bank_interleave(1, 1, 0, False)
         bank_quantize(1, 0, 0)
-        bank_quantize(0, 1, 1)
-        bank_interleave(1, 0, 1, True)
+        bank_interleave(1, 0, 1, H2)
         bank_quantize(1, 1, 0)
+        bank_quantize(0, 1, 1)
         bank_interleave(1, 1, 1, False)
         bank_quantize(1, 0, 1)
         bank_quantize(1, 1, 1)
@@ -396,12 +445,13 @@ def tile_learnedquadraturebankpcensmoother_x2_kernel(
 
         levelled, normalised = set(), set()
         to_normalise, to_turn, to_group, to_quantize = [], [], [], []
-        subtracted = set()
+        subtracted, summed = set(), set()
         step = 0
-        offset_made = []
+        offset_made, quantized = [], []
         while step < UNITS + 4 or scalar_list or to_normalise or to_turn or to_group or to_quantize:
-            turning = to_turn[:VECTOR_RATE]
-            to_turn = to_turn[VECTOR_RATE:]
+            take = VECTOR_RATE if step >= POST_FROM else 0
+            turning = to_turn[:take]
+            to_turn = to_turn[take:]
             if step < UNITS:
                 if step >= 2:
                     project_and_square(step, 0)
@@ -410,11 +460,15 @@ def tile_learnedquadraturebankpcensmoother_x2_kernel(
                 smooth_matmul(step - 3)
             for u in turning:
                 result_transpose(u)
-            if 0 <= step - 1 < UNITS:
-                time_mean(step - 1)
-            if 0 <= step - 2 < UNITS:
+            if step - 1 in projected:
                 c_round(step - 2)
-            if 0 <= step - 1 < UNITS:
+                time_mean(step - 1)
+            else:
+                if 0 <= step - 1 < UNITS:
+                    time_mean(step - 1)
+                if 0 <= step - 2 < UNITS:
+                    c_round(step - 2)
+            if 0 <= step - 1 < TENSOR_SUMS_FROM:
                 deviation(step - 1)
             if 0 <= step - 3 < UNITS:
                 level(step - 3)
@@ -423,15 +477,25 @@ def tile_learnedquadraturebankpcensmoother_x2_kernel(
                 x_transpose(b, g, pair)
             if 0 <= step - 1 < UNITS:
                 dev_transpose(step - 1)
+            if step in projected:
+                vector_copy(step)
             if 0 <= step - 2 < UNITS:
                 c_quantize(step - 2)
+            if step in projected:
+                vector_square(step)
             for b, g, pair in x_pieces_of(step - 1):
                 if pair == 1:
                     x_quantize(b, g)
             for b, h in to_quantize:
                 result_quantize(b, h)
+                quantized.append((b, h))
+                if len(quantized) == 2 * (B - 1):
+                    store_scales(nc.sync, slice(0, (B - 1) * F))
             to_quantize = []
             for u in to_normalise:
+                if u >= TENSOR_SUMS_FROM and u not in summed:
+                    energy(u)
+                    summed.add(u)
                 normalise(u)
                 normalised.add(u)
             to_normalise = []
@@ -446,6 +510,11 @@ def tile_learnedquadraturebankpcensmoother_x2_kernel(
                     result_store(u // FT, (u % FT) // 2)
                     to_group.append((u // FT, (u % FT) // 2))
             band_setup(step - 1)
+            if step == ENERGY_STEP:
+                for u in range(TENSOR_SUMS_FROM, UNITS):
+                    if u not in summed:
+                        energy(u)
+                        summed.add(u)
             if offset_made and step == offset_made[0] + 2:
                 offset_setup()
             budget = SCALAR_RATE if step < UNITS else DRAIN_RATE
@@ -476,8 +545,4 @@ def tile_learnedquadraturebankpcensmoother_x2_kernel(
             for b, g, pair in x_pieces_of(step):
                 x_copy(b, g, pair, step < SCALAR_X_COPIES)
             step = step + 1
-        for quad in range(4):
-            nc.scalar.dma_start(
-                out=out_2[0, 4 * quad : 4 * quad + 4, :].bitcast(I32),
-                in_=out_scales[32 * quad : 32 * quad + 4, :].bitcast(I32),
-            )
+        store_scales(nc.scalar, slice((B - 1) * F, B * F))

from contextlib import ExitStack

import concourse.mybir as mybir
from concourse.masks import make_identity

B, T, L, F = 4, 512, 1024, 512
FLOPS = 2 * B * T * L * F * 2 + 2 * B * T * T * F

F32 = mybir.dt.float32
BF16 = mybir.dt.bfloat16
I32 = mybir.dt.int32
U32 = mybir.dt.uint32
U8 = mybir.dt.uint8
FP8X4 = mybir.dt.float8_e4m3fn_x4
FP4X4 = mybir.dt.float4_e2m1fn_x4
ACT = mybir.ActivationFunctionType
ALU = mybir.AluOpType

P = 128
PACK = 4
PASSES = L // (P * PACK)
FT = F // P
UNITS = B * FT
GROUP_ENDS = (5, 12, 16)
SCALAR_RATE = 2
VECTOR_RATE = 2
SCALAR_X_COPIES = 7
SCALAR_INTERLEAVES = 0
TAIL_ENGINE = (0, 0, 0, 0, 0, 0, 1, 0)
DRAIN_RATE = 2
VECTOR_SQUARES_FROM = 12
POST_FROM = 19
TENSOR_SUMS_FROM = 8
ENERGY_STEP = 21
WARM = (6, 4)
H2 = True
HALF = F // 2


def tile_learnedquadraturebankpcensmoother_x2_kernel(
    tc, x, bank, smoother_words, smoother_scales, tgain, alpha, delta, root, out_0, out_1, out_2
):
    nc = tc.nc
    with ExitStack() as ctx:
        keep = ctx.enter_context(tc.tile_pool(name="keep", bufs=1))
        work = ctx.enter_context(tc.tile_pool(name="work", bufs=3))
        psum = ctx.enter_context(tc.psum_pool(name="psum", bufs=8))
        ctx.enter_context(tc.manual_schedule())

        def kept(name, shape, dtype):
            return keep.tile(shape, dtype, name=name, tag=name, align_bytes=64)

        def passing(name, shape, dtype, bufs):
            return work.tile(shape, dtype, name=name, tag=name, bufs=bufs, align_bytes=64)

        def psum_bank():
            return psum.tile([P, T], F32, name="psum_bank", tag="psum_bank")

        x_raw = {}
        bank_raw = {}

        def load_x(b, pairs):
            rows = x[b].rearrange("(p j) l -> p j l", j=PACK)
            tile = kept("x_raw_%d_%d" % (b, pairs[0]), [P, 2 * len(pairs), L], BF16)
            nc.sync.dma_start(out=tile[:], in_=rows[:, 2 * pairs[0] : 2 * pairs[-1] + 2, :])
            for n, pair in enumerate(pairs):
                x_raw[b, pair] = tile[:, 2 * n : 2 * n + 2, :]

        def load_bank(q, g):
            tile = kept("bank_raw_%d_%d" % (q, g), [P, PACK, F], BF16)
            rows = bank[q, g * P * PACK : (g + 1) * P * PACK, :]
            nc.sync.dma_start(out=tile[:], in_=rows.rearrange("(p j) f -> p j f", j=PACK))
            bank_raw[q, g] = tile

        ident = kept("ident", [P, P], F32)
        make_identity(nc, ident[:])
        w_scales = kept("w_scales", [P, T], U8)
        nc.gpsimd.memset(w_scales[:].bitcast(I32), 0)
        band_rows = kept("band_rows", [P, P], F32)
        nc.gpsimd.memset(band_rows[:], 0.0)
        warm = kept("warm", [P, 1], F32)
        nc.scalar.activation(out=warm[:], in_=ident[:, 0:1], func=ACT.Ln, bias=1.0)

        warm_tile = kept("warm_tile", [P, T], BF16)
        nc.vector.memset(warm_tile[:], 0.0)

        def warm_tensor(count):
            scratch = psum_bank()
            for n in range(count):
                nc.tensor.matmul(scratch[:], lhsT=warm_tile[:, 0:P], rhs=warm_tile[:], start=True, stop=True)

        warm_tensor(WARM[0])
        load_bank(0, 0)
        load_x(0, [0])
        load_x(0, [1])
        load_bank(0, 1)
        load_bank(1, 0)
        load_bank(1, 1)
        load_x(1, [0, 1])
        gain_raw = kept("gain_raw", [P, PACK], BF16)
        nc.sync.dma_start(out=gain_raw[:], in_=tgain.rearrange("(p j) -> p j", j=PACK))
        w_words = kept("w_words", [P, 2 * T], U8)
        nc.sync.dma_start(out=w_words[:].bitcast(I32), in_=smoother_words[0].bitcast(I32))
        for quad in range(4):
            nc.sync.dma_start(
                out=w_scales[32 * quad : 32 * quad + 4, :].bitcast(I32),
                in_=smoother_scales[0, 4 * quad : 4 * quad + 4, :].bitcast(I32),
            )
        band_raw = kept("band_raw", [3 * FT, P], BF16)
        for n, vec in enumerate((alpha, delta, root)):
            nc.sync.dma_start(out=band_raw[FT * n : FT * (n + 1), :], in_=vec.rearrange("(c m) -> c m", m=P))
        load_x(2, [0, 1])
        load_x(3, [0, 1])

        bank_codes, bank_scales, bank_grouped = {}, {}, {}

        def interleave(grouped, src, on_scalar):
            dst = grouped[:].rearrange("p (c i) j -> p c j i", i=4)
            src = src.rearrange("p j (c i) -> p c j i", i=4)
            if on_scalar == 2:
                nc.gpsimd.tensor_scalar(out=dst, in0=src, scalar1=1.0, scalar2=0.0, op0=ALU.mult, op1=ALU.add)
            elif on_scalar:
                nc.scalar.copy(out=dst, in_=src)
            else:
                nc.vector.tensor_copy(out=dst, in_=src)

        def bank_interleave(q, g, h, on_scalar):
            grouped = passing("bank_grouped", [P, HALF, PACK], BF16, 5)
            interleave(grouped, bank_raw[q, g][:, :, h * HALF : (h + 1) * HALF], on_scalar)
            bank_grouped[q, g, h] = grouped

        def bank_quantize(q, g, h):
            codes = kept("bank_codes_%d_%d_%d" % (q, g, h), [P, HALF], U32)
            scales = kept("bank_scales_%d_%d_%d" % (q, g, h), [P, HALF], U8)
            nc.vector.quantize_mx(
                out=codes[:].bitcast(FP8X4),
                scales=scales[:],
                in_=bank_grouped[q, g, h][:].rearrange("p c j -> p (c j)"),
            )
            bank_codes[q, g, h], bank_scales[q, g, h] = codes, scales

        x_turned, x_grouped, x_codes, x_scales = {}, {}, {}, {}

        def x_transpose(b, g, pair):
            turned = psum_bank()
            for jj in range(2):
                words = x_raw[b, pair][:, jj, :].bitcast(F32)
                for u in range(2):
                    slot = 2 * jj + u
                    nc.tensor.transpose(
                        turned[:, slot * P : (slot + 1) * P],
                        words[:, 2 * P * g + u : 2 * P * (g + 1) : 2],
                        ident[:],
                    )
            x_turned[b, g, pair] = turned

        def x_copy(b, g, pair, on_scalar):
            if pair == 0:
                x_grouped[b, g] = passing("x_grouped", [P, T * PACK], BF16, 3)
            words = x_grouped[b, g][:].bitcast(F32)
            dst = words[:, pair * T : (pair + 1) * T].rearrange("p (j r u) -> p j r u", j=2, u=2)
            src = x_turned[b, g, pair][:].rearrange("p (j u r) -> p j r u", j=2, u=2)
            if on_scalar:
                nc.scalar.copy(out=dst, in_=src)
            else:
                nc.vector.tensor_copy(out=dst, in_=src)

        def x_quantize(b, g):
            codes = kept("x_codes_%d_%d" % (b, g), [P, T], U32)
            scales = kept("x_scales_%d_%d" % (b, g), [P, T], U8)
            nc.vector.quantize_mx(out=codes[:].bitcast(FP8X4), scales=scales[:], in_=x_grouped[b, g][:])
            x_codes[b, g], x_scales[b, g] = codes, scales

        dev = [kept("dev_%d" % ft, [P, B, T], F32) for ft in range(FT)]
        chain = [kept("chain_%d" % ft, [P, B, T], F32) for ft in range(FT)]

        def of_unit(tiles, u):
            b, ft = divmod(u, FT)
            return tiles[ft][:, b, :]

        sums = kept("sums", [P, UNITS, 2], F32)
        neg_mean = kept("neg_mean", [P, UNITS], F32)
        vector_sums = kept("vector_sums", [P, UNITS], F32)
        squares, projected, plain = {}, {}, {}

        def project_and_square(u, q):
            b, ft = divmod(u, FT)
            h, cols = ft // 2, slice((ft % 2) * P, (ft % 2 + 1) * P)
            z = psum_bank()
            for g in range(PASSES):
                nc.tensor.matmul_mx(
                    out=z[:],
                    lhsT=bank_codes[q, g, h][:, cols].bitcast(FP8X4),
                    lhsT_scale=bank_scales[q, g, h][:, cols],
                    rhs=x_codes[b, g][:].bitcast(FP8X4),
                    rhs_scale=x_scales[b, g][:],
                    start=(g == 0),
                    stop=(g == PASSES - 1),
                )
            if u < TENSOR_SUMS_FROM:
                square = passing("square_%d" % q, [P, T], F32, 3)[:]
            elif q == 0:
                square = of_unit(dev, u)
            else:
                square = kept("late_square_%d" % u, [P, T], F32)[:]
            if q == 1 and u >= VECTOR_SQUARES_FROM:
                projected[u] = z
            else:
                nc.scalar.activation(out=square, in_=z[:], func=ACT.Square, accum_out=sums[:, u, q : q + 1])
            squares[u, q] = square

        def vector_copy(u):
            plain[u] = passing("plain", [P, T], F32, 2)
            nc.vector.tensor_copy(out=plain[u][:], in_=projected[u][:])

        def vector_square(u):
            nc.vector.scalar_tensor_tensor(
                out=squares[u, 1], in0=projected[u][:], scalar=1.0, in1=plain[u][:], op0=ALU.mult, op1=ALU.mult,
                accum_out=vector_sums[:, u : u + 1],
            )

        def time_mean(u):
            nc.vector.tensor_scalar(
                out=neg_mean[:, u : u + 1], in0=sums[:, u, 0:1], scalar1=vector_sums[:, u : u + 1] if u >= VECTOR_SQUARES_FROM else sums[:, u, 1:2], scalar2=-1.0 / T,
                op0=ALU.add, op1=ALU.mult,
            )

        def deviation(u):
            nc.vector.scalar_tensor_tensor(
                out=of_unit(dev, u), in0=squares[u, 0], scalar=neg_mean[:, u : u + 1], in1=squares[u, 1],
                op0=ALU.add, op1=ALU.add,
            )

        dev_turned, c_grouped, c_codes, c_scales, smooth = {}, {}, {}, {}, {}

        def turn(src):
            turned = psum_bank()
            for j in range(PACK):
                nc.tensor.transpose(turned[:, j * P : (j + 1) * P], src[:, j * P : (j + 1) * P], ident[:])
            return turned

        def dev_transpose(u):
            if u < TENSOR_SUMS_FROM:
                dev_turned[u] = turn(of_unit(dev, u))
                return
            dev_turned[u] = psum_bank()
            for j in range(PACK):
                cols = slice(j * P, (j + 1) * P)
                terms = (squares[u, 0][:, cols], squares[u, 1][:, cols], neg_mean[:, u : u + 1].to_broadcast([P, P]))
                for n, term in enumerate(terms):
                    nc.tensor.matmul(
                        dev_turned[u][:, cols], lhsT=term, rhs=ident[:], is_transpose=True,
                        start=(n == 0), stop=(n == len(terms) - 1),
                    )

        gain = gain_raw[:].unsqueeze(1).to_broadcast([P, P, PACK])

        def c_round(u):
            grouped = passing("c_grouped", [P, P, PACK], BF16, 3)
            nc.vector.tensor_tensor(
                out=grouped[:], in0=dev_turned[u][:].rearrange("p (j f) -> p f j", j=PACK), in1=gain, op=ALU.mult
            )
            c_grouped[u] = grouped

        def c_quantize(u):
            codes = passing("c_codes", [P, P], U32, 3)
            scales = passing("c_scales", [P, P], U8, 3)
            nc.vector.quantize_mx(
                out=codes[:].bitcast(FP8X4), scales=scales[:], in_=c_grouped[u][:].rearrange("p f j -> p (f j)")
            )
            c_codes[u], c_scales[u] = codes, scales

        def smooth_matmul(u):
            sm = psum_bank()
            nc.tensor.matmul_mx(
                out=sm[:], lhsT=c_codes[u][:].bitcast(FP8X4), lhsT_scale=c_scales[u][:],
                rhs=w_words[:].bitcast(FP4X4), rhs_scale=w_scales[:], start=True, stop=True,
            )
            smooth[u] = sm

        def level(u):
            nc.vector.tensor_scalar(
                out=of_unit(chain, u).rearrange("f (j p) -> f j p", j=PACK),
                in0=smooth[u][:].rearrange("f (p j) -> f j p", j=PACK),
                scalar1=neg_mean[:, u : u + 1], scalar2=0.1, op0=ALU.subtract, op1=ALU.max,
            )

        def log_level(u):
            nc.scalar.activation(out=of_unit(chain, u), in_=of_unit(chain, u), func=ACT.Ln, bias=0.01)

        band = kept("band", [P, 3 * FT], F32)
        neg_alpha = kept("neg_alpha", [P, FT], F32)
        log_delta = kept("log_delta", [P, FT], F32)
        root_log_delta = kept("root_log_delta", [P, FT], F32)
        offset_col = kept("offset_col", [P, FT], F32)
        offset_row = kept("offset_row", [P, F], F32)

        band_turned = []

        def band_setup(stage):
            if stage == 0:
                nc.vector.tensor_copy(out=band_rows[0 : 3 * FT, :], in_=band_raw[:])
            if stage == 1:
                band_turned.append(psum_bank())
                nc.tensor.transpose(band_turned[0][:, 0:P], band_rows[:], ident[:])
            if stage == 2:
                nc.vector.tensor_copy(out=band[:], in_=band_turned[0][:, 0 : 3 * FT])
            if stage == 3:
                nc.scalar.activation(out=log_delta[:], in_=band[:, FT : 2 * FT], func=ACT.Ln)
                nc.vector.tensor_scalar(out=neg_alpha[:], in0=band[:, 0:FT], scalar1=-1.0, scalar2=None, op0=ALU.mult)
            if stage == 4:
                nc.vector.tensor_tensor(
                    out=root_log_delta[:], in0=log_delta[:], in1=band[:, 2 * FT : 3 * FT], op=ALU.mult
                )

        def offset_setup():
            turned = psum_bank()
            for ft in range(FT):
                nc.tensor.transpose(
                    turned[:, ft * P : (ft + 1) * P], offset_col[:, ft : ft + 1].to_broadcast([P, P]), ident[:]
                )
            nc.vector.tensor_copy(out=offset_row[:], in_=turned[:])

        def chain_of(units):
            return chain[units[0] % FT][:, units[0] // FT : units[-1] // FT + 1, :]

        def inverse_power(units):
            ft = units[0] % FT
            nc.scalar.activation(out=chain_of(units), in_=chain_of(units), func=ACT.Exp, scale=neg_alpha[:, ft : ft + 1])

        def energy(u):
            nc.vector.tensor_tensor(out=of_unit(dev, u), in0=of_unit(dev, u), in1=squares[u, 1], op=ALU.add)

        def normalise(u):
            if u >= TENSOR_SUMS_FROM:
                nc.vector.tensor_tensor(out=of_unit(chain, u), in0=of_unit(dev, u), in1=of_unit(chain, u), op=ALU.mult)
            else:
                nc.vector.scalar_tensor_tensor(
                    out=of_unit(chain, u), in0=of_unit(dev, u), scalar=neg_mean[:, u : u + 1], in1=of_unit(chain, u),
                    op0=ALU.subtract, op1=ALU.mult,
                )

        def log_shifted(units):
            col = FT + units[0] % FT
            nc.scalar.activation(out=chain_of(units), in_=chain_of(units), func=ACT.Ln, bias=band[:, col : col + 1])

        def root_power(units):
            col = 2 * FT + units[0] % FT
            nc.scalar.activation(out=chain_of(units), in_=chain_of(units), func=ACT.Exp, scale=band[:, col : col + 1])

        result, result_turned, result_grouped = {}, {}, {}
        out_scales = kept("out_scales", [P, B * F], U8)
        out_words = out_1[0].rearrange("p m t -> p (m t)").bitcast(I32)

        def result_transpose(u):
            result_turned[u] = turn(of_unit(chain, u))

        def result_subtract(u):
            b, ft = divmod(u, FT)
            if (b, ft // 2) not in result:
                result[b, ft // 2] = passing("result", [P, PACK, HALF], F32, 4)
            nc.vector.tensor_tensor(
                out=result[b, ft // 2][:, :, (ft % 2) * P : (ft % 2 + 1) * P],
                in0=result_turned[u][:].rearrange("p (j f) -> p j f", j=PACK),
                in1=offset_row[:, ft * P : (ft + 1) * P].unsqueeze(1).to_broadcast([P, PACK, P]),
                op=ALU.subtract,
            )

        def result_store(b, h):
            rows = out_0[b].rearrange("(p j) f -> p j f", j=PACK)
            nc.sync.dma_start(out=rows[:, :, h * HALF : (h + 1) * HALF], in_=result[b, h][:])

        def result_interleave(b, h, on_scalar):
            grouped = passing("result_grouped", [P, HALF, PACK], BF16, 3)
            interleave(grouped, result[b, h][:], on_scalar)
            result_grouped[b, h] = grouped

        def result_quantize(b, h):
            cols = slice(b * F + h * HALF, b * F + (h + 1) * HALF)
            codes = passing("result_codes", [P, HALF], U32, 4)
            nc.vector.quantize_mx(
                out=codes[:].bitcast(FP8X4), scales=out_scales[:, cols],
                in_=result_grouped[b, h][:].rearrange("p c j -> p (c j)"),
            )
            nc.sync.dma_start(out=out_words[:, cols], in_=codes[:].bitcast(I32))

        def store_scales(queue, cols):
            for quad in range(4):
                queue.dma_start(
                    out=out_2[0, 4 * quad : 4 * quad + 4, cols].bitcast(I32),
                    in_=out_scales[32 * quad : 32 * quad + 4, cols].bitcast(I32),
                )

        for h in range(2):
            bank_interleave(0, 0, h, False)
        for h in range(2):
            bank_quantize(0, 0, h)
        for pair in range(2):
            for g in range(PASSES):
                x_transpose(0, g, pair)
                x_copy(0, g, pair, True)
        warm_tensor(WARM[1])
        bank_interleave(0, 1, 0, False)
        bank_interleave(0, 1, 1, True)
        x_quantize(0, 0)
        bank_quantize(0, 1, 0)
        x_quantize(0, 1)
        project_and_square(0, 0)
        project_and_square(1, 0)
        bank_interleave(1, 0, 0, False)
        bank_interleave(1, 1, 0, False)
        bank_quantize(1, 0, 0)
        bank_interleave(1, 0, 1, H2)
        bank_quantize(1, 1, 0)
        bank_quantize(0, 1, 1)
        bank_interleave(1, 1, 1, False)
        bank_quantize(1, 0, 1)
        bank_quantize(1, 1, 1)
        x_pieces = [(b, g, pair) for b in range(1, B) for g in range(PASSES) for pair in range(2)]

        def x_pieces_of(step):
            return [piece for n, piece in enumerate(x_pieces) if (1 + n // 2 if n < 4 else n - 1) == step]

        groups = [list(range(lo, hi)) for lo, hi in zip((0,) + GROUP_ENDS[:-1], GROUP_ENDS)]

        def runs(units, width):
            found = []
            for first in range(units[0] // FT, B, width):
                for ft in range(FT):
                    run = [u for u in units if u % FT == ft and first <= u // FT < first + width]
                    if run:
                        found.append(run)
            return found

        scalar_list = []
        for n in range(len(groups) + 1):
            if n < len(groups):
                scalar_list.extend(("log_level", [u]) for u in groups[n])
            if n >= 1:
                scalar_list.extend(("log_shifted", run) for run in runs(groups[n - 1], 2))
            if n < len(groups):
                scalar_list.extend(("inverse_power", run) for run in runs(groups[n], 2))
            if n >= 1:
                scalar_list.extend(("root_power", run) for run in runs(groups[n - 1], 1 if n == len(groups) else 2))

        levelled, normalised = set(), set()
        to_normalise, to_turn, to_group, to_quantize = [], [], [], []
        subtracted, summed = set(), set()
        step = 0
        offset_made, quantized = [], []
        while step < UNITS + 4 or scalar_list or to_normalise or to_turn or to_group or to_quantize:
            take = VECTOR_RATE if step >= POST_FROM else 0
            turning = to_turn[:take]
            to_turn = to_turn[take:]
            if step < UNITS:
                if step >= 2:
                    project_and_square(step, 0)
                project_and_square(step, 1)
            if 0 <= step - 3 < UNITS:
                smooth_matmul(step - 3)
            for u in turning:
                result_transpose(u)
            if step - 1 in projected:
                c_round(step - 2)
                time_mean(step - 1)
            else:
                if 0 <= step - 1 < UNITS:
                    time_mean(step - 1)
                if 0 <= step - 2 < UNITS:
                    c_round(step - 2)
            if 0 <= step - 1 < TENSOR_SUMS_FROM:
                deviation(step - 1)
            if 0 <= step - 3 < UNITS:
                level(step - 3)
                levelled.add(step - 3)
            for b, g, pair in x_pieces_of(step):
                x_transpose(b, g, pair)
            if 0 <= step - 1 < UNITS:
                dev_transpose(step - 1)
            if step in projected:
                vector_copy(step)
            if 0 <= step - 2 < UNITS:
                c_quantize(step - 2)
            if step in projected:
                vector_square(step)
            for b, g, pair in x_pieces_of(step - 1):
                if pair == 1:
                    x_quantize(b, g)
            for b, h in to_quantize:
                result_quantize(b, h)
                quantized.append((b, h))
                if len(quantized) == 2 * (B - 1):
                    store_scales(nc.sync, slice(0, (B - 1) * F))
            to_quantize = []
            for u in to_normalise:
                if u >= TENSOR_SUMS_FROM and u not in summed:
                    energy(u)
                    summed.add(u)
                normalise(u)
                normalised.add(u)
            to_normalise = []
            for b, h in to_group:
                result_interleave(b, h, TAIL_ENGINE[2 * b + h])
                to_quantize.append((b, h))
            to_group = []
            for u in turning:
                result_subtract(u)
                subtracted.add(u)
                if u ^ 1 in subtracted:
                    result_store(u // FT, (u % FT) // 2)
                    to_group.append((u // FT, (u % FT) // 2))
            band_setup(step - 1)
            if step == ENERGY_STEP:
                for u in range(TENSOR_SUMS_FROM, UNITS):
                    if u not in summed:
                        energy(u)
                        summed.add(u)
            if offset_made and step == offset_made[0] + 2:
                offset_setup()
            budget = SCALAR_RATE if step < UNITS else DRAIN_RATE
            while scalar_list and budget > 0:
                at = 0
                while scalar_list[at][0] == "log_level" and scalar_list[at][1][0] not in levelled:
                    at = at + 1
                kind, run = scalar_list[at]
                if at > 0 and kind != "log_shifted":
                    break
                if kind == "log_level":
                    log_level(run[0])
                elif kind == "inverse_power":
                    if not offset_made:
                        nc.scalar.activation(out=offset_col[:], in_=root_log_delta[:], func=ACT.Exp)
                        offset_made.append(step)
                    inverse_power(run)
                    to_normalise.extend(run)
                elif kind == "log_shifted":
                    if not all(u in normalised for u in run):
                        break
                    log_shifted(run)
                else:
                    root_power(run)
                    to_turn.extend(run)
                budget = budget - len(run)
                scalar_list = scalar_list[:at] + scalar_list[at + 1 :]
            for b, g, pair in x_pieces_of(step):
                x_copy(b, g, pair, step < SCALAR_X_COPIES)
            step = step + 1
        store_scales(nc.scalar, slice((B - 1) * F, B * F))
